import numpy as np, ml_dtypes
CORES = [2,3,42,43,82,83,122,123]
N = 8
import mx_ref
NC, KT, G, WT = 256, 1, 2, 1
C = np.float32(0.031)
BF = ml_dtypes.bfloat16
def cut(t, i, w=512):
    return t[:, w * i:w * i + w]
def tile(rs):
    return np.stack(rs, axis=2).reshape(128, -1).astype(BF)
def layer(w, X):
    out = []
    for i in range(G):
        for t in range(len(X)):
            p = mx_ref.matmul(mx_ref.quantize(cut(w, len(X) * i + t)), X[t])
            z = p if t == 0 else z + p
        out.append(z)
    return out
def act(Z):
    return [np.maximum(s * z, 0) * C for z in Z for s in (1, -1)]
def setup_inputs(rng):
    def f(*shape):
        return mx_ref.flush((rng.standard_normal(shape, dtype=np.float32) * np.exp2(rng.integers(-2, 3, shape[:-1] + (1,)))).astype(BF))
    return {"x": f(N, 128, KT * 4 * NC), "w1": f(N, 128, G * KT * 512), "w2": f(N, 128, WT * 512)}
def setup_inputs_blocks(rng):
    d = setup_inputs(rng)
    for k in ("x", "w1", "w2"): d[k] = mx_ref.spread(d[k], rng, 4)
    return d
def setup_inputs_wide(rng):
    d = setup_inputs(rng)
    for k in ("x", "w1", "w2"): d[k] = mx_ref.flush((d[k].astype(np.float32) * np.exp2(rng.integers(-8, 9, (N, 1, 1))).astype(np.float32)).astype(BF))
    return d
def setup_inputs_zeros(rng):
    d = setup_inputs(rng); v = d["x"].reshape(N, 128, -1, 4).copy()
    v[np.broadcast_to((rng.random((N, 1, v.shape[2], 1)) < 0.33), v.shape)] = 0
    d["x"] = v.reshape(d["x"].shape)
    return d
def reference(x, w1, w2):
    H = [mx_ref.quantize(tile(act(layer(w1[j], [mx_ref.quantize(cut(x[j], t, 4 * NC)) for t in range(KT)])))) for j in range(N)]
    y = np.zeros((N, 128, N * WT * NC), np.float32)
    for r in range(N):
        for i in range(WT):
            qw = mx_ref.quantize(cut(w2[r], i))
            for j in range(N):
                y[r][:, NC * (WT * j + i):NC * (WT * j + i) + NC] = mx_ref.matmul(qw, H[j])
    return {"y": y}

@@ -1,0 +1,162 @@
+from concourse.mybir import dt, AluOpType, ActivationFunctionType
+
+N = 8
+NC = 256
+CF = 0.031
+
+SCRATCH = {
+    "xb": ("sbuf", [128, 4 * NC], "bfloat16"),
+    "w1b": ("sbuf", [128, 1024], "bfloat16"),
+    "w2b": ("sbuf", [128, 512], "bfloat16"),
+    "xq": ("sbuf", [128, NC], "float8_e4m3fn_x4"),
+    "xs": ("sbuf", [128, NC], "uint8"),
+    "w1q": ("sbuf", [128, 256], "float8_e4m3fn_x4"),
+    "w1s": ("sbuf", [128, 256], "uint8"),
+    "w2q": ("sbuf", [128, 128], "float8_e4m3fn_x4"),
+    "w2s": ("sbuf", [128, 128], "uint8"),
+    "hb": ("sbuf", [128, 4 * NC], "bfloat16"),
+    "hq": ("sbuf", [128, N * NC], "float8_e4m3fn_x4"),
+    "hs": ("sbuf", [128, N * NC], "uint8"),
+    "yb": ("sbuf", [128, N * NC], "float32"),
+    "ps": ("psum", [128, 512 * 8], "float32"),
+}
+SEMAPHORES = (["ldx", "ldw1", "ldw2", "qx", "qw1a", "qw1b", "qw2", "z0", "z1", "av", "as_", "hdone", "sent", "st"]
+              + ["c%d" % j for j in range(N)] + ["p%d" % j for j in range(N)]
+              + ["m%d" % j for j in range(N)] + ["e%d" % j for j in range(N)])
+
+
+def _bits(m):
+    return bin(m).count("1")
+
+
+def _plan(T, topo):
+    cores = list(T.cores)
+    chips = []
+    for c in cores:
+        if topo.chip(c) not in chips:
+            chips.append(topo.chip(c))
+    mem = [[c for c in cores if topo.chip(c) == ch] for ch in chips]
+    K = len(chips)
+    sends = {c: [] for c in cores}
+    order = {c: [] for c in cores}
+    for k in range(K):
+        for s, c in enumerate(mem[k]):
+            other = mem[k][1 - s]
+            me = T.rank_of(c)
+            for d in range(1, K):
+                sends[c].append((me, mem[(k + d) % K][s]))
+            sends[c].append((me, other))
+            order[c] += [me, T.rank_of(other)]
+            for d in range(1, K):
+                src = mem[(k - d) % K]
+                sends[c].append((T.rank_of(src[s]), other))
+                order[c] += [T.rank_of(src[s]), T.rank_of(src[1 - s])]
+    return sends, order
+
+
+def _mask(topo, cores, src, dst):
+    full = topo.mask(src, dst)
+    if topo.chip(src) != topo.chip(dst):
+        return full
+    far = 0
+    for c in cores:
+        if topo.chip(c) != topo.chip(src):
+            far |= topo.mask(src, c)
+    rest = full & ~far
+    return rest if _bits(rest) in (1, 2, 4, 8, 16) else full
+
+
+def rank_program(g, core, T, topo):
+    rank = T.rank_of(core)
+    if rank is None:
+        return
+    S = T.sem
+    sends, order = _plan(T, topo)
+    cores = list(T.cores)
+    got = {}
+    for c in cores:
+        for j, dst in sends[c]:
+            if dst == core:
+                got[j] = _bits(_mask(topo, cores, c, dst))
+
+    def blk(j):
+        return slice(NC * j, NC * j + NC)
+
+    v, sc, te, sy = g.vector, g.scalar, g.tensor, g.sync
+
+    sy.dma_start(T.xb[:], T.x[:]).then_inc(S.ldx, 16)
+    sc.dma_start(T.w1b[:], T.w1[:]).then_inc(S.ldw1, 16)
+    sy.dma_start(T.w2b[:], T.w2[:]).then_inc(S.ldw2, 16)
+
+    v.wait_ge(S.ldx, 16)
+    v.quantize_mx(T.xq[:], T.xs[:], T.xb[:]).then_inc(S.qx, 1)
+    v.wait_ge(S.ldw1, 16)
+    v.quantize_mx(T.w1q[:, 0:128], T.w1s[:, 0:128], T.w1b[:, 0:512]).then_inc(S.qw1a, 1)
+    v.quantize_mx(T.w1q[:, 128:256], T.w1s[:, 128:256], T.w1b[:, 512:1024]).then_inc(S.qw1b, 1)
+    v.wait_ge(S.z0, 1)
+    v.tensor_scalar(T.hb[:, 0:4 * NC:4], T.ps[:, 0:NC], 0.0, CF, AluOpType.max, AluOpType.mult).then_inc(S.av, 1)
+    v.tensor_scalar(T.hb[:, 1:4 * NC:4], T.ps[:, 0:NC], -CF, 0.0, AluOpType.mult, AluOpType.max).then_inc(S.av, 1)
+    v.wait_ge(S.av, 2)
+    v.wait_ge(S.as_, 2)
+    v.quantize_mx(T.hq[:, blk(rank)], T.hs[:, blk(rank)], T.hb[:]).then_inc(S.hdone, 1)
+    v.wait_ge(S.ldw2, 16)
+    v.quantize_mx(T.w2q[:], T.w2s[:], T.w2b[:]).then_inc(S.qw2, 1)
+
+    sc.wait_ge(S.z1, 1)
+    sc.activation(T.hb[:, 2:4 * NC:4], T.ps[:, 512:512 + NC], ActivationFunctionType.Relu, scale=CF).then_inc(S.as_, 1)
+    sc.activation(T.hb[:, 3:4 * NC:4], T.ps[:, 512:512 + NC], ActivationFunctionType.Relu, scale=-CF).then_inc(S.as_, 1)
+
+    te.wait_ge(S.qx, 1)
+    te.wait_ge(S.qw1a, 1)
+    te.matmul_mx(T.ps[:, 0:NC], T.w1q[:, 0:128], T.w1s[:, 0:128], T.xq[:], T.xs[:], True, True).then_inc(S.z0, 1)
+    te.wait_ge(S.qw1b, 1)
+    te.matmul_mx(T.ps[:, 512:512 + NC], T.w1q[:, 128:256], T.w1s[:, 128:256], T.xq[:], T.xs[:], True, True).then_inc(S.z1, 1)
+    te.wait_ge(S.hdone, 1)
+    te.wait_ge(S.qw2, 1)
+    seq = order[core]
+    bank = {}
+    for i, j in enumerate(seq):
+        bank[j] = 512 * ((2 + i) % 8)
+        if j != rank:
+            te.wait_ge(S["p%d" % j], got[j])
+            te.wait_ge(S["c%d" % j], got[j])
+        te.matmul_mx(T.ps[:, bank[j]:bank[j] + NC], T.w2q[:], T.w2s[:], T.hq[:, blk(j)], T.hs[:, blk(j)],
+                     True, True).then_inc(S["m%d" % j], 1)
+
+    for i, j in enumerate(seq):
+        if i % 2 == 0:
+            v.wait_ge(S["m%d" % j], 1)
+            v.tensor_copy(T.yb[:, blk(j)], T.ps[:, bank[j]:bank[j] + NC]).then_inc(S["e%d" % j], 1)
+        else:
+            sc.wait_ge(S["m%d" % j], 1)
+            sc.activation(T.yb[:, blk(j)], T.ps[:, bank[j]:bank[j] + NC], ActivationFunctionType.Copy).then_inc(S["e%d" % j], 1)
+
+    nst = 0
+    for i in range(0, N, 2):
+        a, b = seq[i], seq[i + 1]
+        lo = min(a, b)
+        if i + 2 < N and abs(a - b) == 1:
+            sy.wait_ge(S["e%d" % a], 1)
+            sy.wait_ge(S["e%d" % b], 1)
+            sy.dma_start(T.y[:, NC * lo:NC * lo + 2 * NC], T.yb[:, NC * lo:NC * lo + 2 * NC]).then_inc(S.st, 16)
+            nst += 1
+        else:
+            for j in (a, b):
+                sy.wait_ge(S["e%d" % j], 1)
+                sy.dma_start(T.y[:, blk(j)], T.yb[:, blk(j)]).then_inc(S.st, 16)
+                nst += 1
+    sy.wait_ge(S.st, 16 * nst)
+
+    g.wait_ge(S.hdone, 1)
+    total = 0
+    for j, dst in sends[core]:
+        m = _mask(topo, cores, core, dst)
+        rid, pid, _se = topo.addr(dst)
+        if j != rank:
+            g.wait_ge(S["p%d" % j], got[j])
+        g.remote_dma(T.hs[:, blk(j)], T.hs[:, blk(j)], S["p%d" % j], S.sent, pid, rid, m)
+        if j != rank:
+            g.wait_ge(S["c%d" % j], got[j])
+        g.remote_dma(T.hq[:, blk(j)].bitcast(dt.uint8), T.hq[:, blk(j)].bitcast(dt.uint8), S["c%d" % j], S.sent, pid, rid, m)
+        total += 2 * _bits(m)
+    g.wait_ge(S.sent, total)

@@ -2,7 +2,10 @@ from concourse.mybir import dt, AluOpType, ActivationFunctionType
 
 N = 8
 NC = 256
+HC = NC // 2
 CF = 0.031
+DIRECT = ()
+HELP = (3,)
 
 SCRATCH = {
     "xb": ("sbuf", [128, 4 * NC], "bfloat16"),
@@ -20,13 +23,26 @@ SCRATCH = {
     "yb": ("sbuf", [128, N * NC], "float32"),
     "ps": ("psum", [128, 512 * 8], "float32"),
 }
-SEMAPHORES = (["ldx", "ldw1", "ldw2", "qx", "qw1a", "qw1b", "qw2", "z0", "z1", "av", "as_", "hdone", "sent", "st"]
+SEMAPHORES = (["ldx", "ldw1", "ldw2", "qx0", "qx1", "qw1a", "qw1b", "qw2", "z00", "z10", "z01", "z11",
+               "av0", "av1", "as0", "as1", "h0", "h1", "sent", "st"]
               + ["c%d" % j for j in range(N)] + ["p%d" % j for j in range(N)]
               + ["m%d" % j for j in range(N)] + ["e%d" % j for j in range(N)])
 
 
 def _bits(m):
     return bin(m).count("1")
+
+
+def _masks(topo, cores, src, dst):
+    full = topo.mask(src, dst)
+    if topo.chip(src) != topo.chip(dst):
+        return full, full
+    far = 0
+    for c in cores:
+        if topo.chip(c) != topo.chip(src):
+            far |= topo.mask(src, c)
+    rest = full & ~far
+    return (rest if _bits(rest) in (1, 2, 4, 8, 16) else full), full
 
 
 def _plan(T, topo):
@@ -37,89 +53,136 @@ def _plan(T, topo):
             chips.append(topo.chip(c))
     mem = [[c for c in cores if topo.chip(c) == ch] for ch in chips]
     K = len(chips)
-    sends = {c: [] for c in cores}
+    ops = {c: [] for c in cores}
     order = {c: [] for c in cores}
+
+    def both(lst, j, src, dst, split=False):
+        m = _masks(topo, cores, src, dst)[0]
+        if split:
+            lst.append(("p", j, 0, HC, dst, m))
+            lst.append(("p", j, HC, NC, dst, m))
+        else:
+            lst.append(("p", j, 0, NC, dst, m))
+        lst.append(("c", j, 0, NC, dst, m))
+
     for k in range(K):
         for s, c in enumerate(mem[k]):
             other = mem[k][1 - s]
             me = T.rank_of(c)
+            hc = None
+            if HELP:
+                cand = [q for q in range(128) if topo.chip(q) == chips[k] and q not in cores and topo.die(q) != topo.die(c)
+                        and all(topo.may_write(q, t) for t in cores)]
+                hc = cand[s]
+                both(ops[c], me, c, hc, True)
+                ops[hc] = []
             for d in range(1, K):
-                sends[c].append((me, mem[(k + d) % K][s]))
-            sends[c].append((me, other))
+                who = hc if d in HELP else c
+                both(ops[who], me, who, mem[(k + d) % K][s])
+                if d in DIRECT:
+                    both(ops[who], me, who, mem[(k + d) % K][1 - s])
+            both(ops[c], me, c, other)
             order[c] += [me, T.rank_of(other)]
             for d in range(1, K):
                 src = mem[(k - d) % K]
-                sends[c].append((T.rank_of(src[s]), other))
-                order[c] += [T.rank_of(src[s]), T.rank_of(src[1 - s])]
-    return sends, order
-
-
-def _mask(topo, cores, src, dst):
-    full = topo.mask(src, dst)
-    if topo.chip(src) != topo.chip(dst):
-        return full
-    far = 0
-    for c in cores:
-        if topo.chip(c) != topo.chip(src):
-            far |= topo.mask(src, c)
-    rest = full & ~far
-    return rest if _bits(rest) in (1, 2, 4, 8, 16) else full
+                j = T.rank_of(src[s])
+                if d not in DIRECT:
+                    both(ops[c], j, c, other)
+                order[c] += [j, T.rank_of(src[1 - s])]
+    return ops, order
 
 
 def rank_program(g, core, T, topo):
     rank = T.rank_of(core)
-    if rank is None:
-        return
     S = T.sem
-    sends, order = _plan(T, topo)
-    cores = list(T.cores)
+    ops, order = _plan(T, topo)
+    if core not in ops:
+        return
     got = {}
-    for c in cores:
-        for j, dst in sends[c]:
+    for c in ops:
+        for kind, j, a, b, dst, m in ops[c]:
             if dst == core:
-                got[j] = _bits(_mask(topo, cores, c, dst))
+                got[kind, j] = got.get((kind, j), 0) + _bits(m)
+    if rank is not None:
+        _compute(g, rank, T, order[core], got)
+
+    total = 0
+    seen = set()
+    for kind, j, a, b, dst, m in ops[core]:
+        if j == rank:
+            need = [("h0", 1)] if b <= HC else [("h0", 1), ("h1", 1)]
+        else:
+            need = [("%s%d" % (kind, j), got[kind, j])]
+        for name, val in need:
+            if name not in seen:
+                g.wait_ge(S[name], val)
+                seen.add(name)
+        rid, pid, _se = topo.addr(dst)
+        cols = slice(NC * j + a, NC * j + b)
+        if kind == "p":
+            g.remote_dma(T.hs[:, cols], T.hs[:, cols], S["p%d" % j], S.sent, pid, rid, m)
+        else:
+            g.remote_dma(T.hq[:, cols].bitcast(dt.uint8), T.hq[:, cols].bitcast(dt.uint8), S["c%d" % j], S.sent, pid, rid, m)
+        total += _bits(m)
+    g.wait_ge(S.sent, total)
+
+
+def _compute(g, rank, T, seq, got):
+    S = T.sem
 
     def blk(j):
         return slice(NC * j, NC * j + NC)
 
     v, sc, te, sy = g.vector, g.scalar, g.tensor, g.sync
+    Relu, Copy = ActivationFunctionType.Relu, ActivationFunctionType.Copy
 
     sy.dma_start(T.xb[:], T.x[:]).then_inc(S.ldx, 16)
     sc.dma_start(T.w1b[:], T.w1[:]).then_inc(S.ldw1, 16)
     sy.dma_start(T.w2b[:], T.w2[:]).then_inc(S.ldw2, 16)
 
     v.wait_ge(S.ldx, 16)
-    v.quantize_mx(T.xq[:], T.xs[:], T.xb[:]).then_inc(S.qx, 1)
+    v.quantize_mx(T.xq[:, 0:HC], T.xs[:, 0:HC], T.xb[:, 0:4 * HC]).then_inc(S.qx0, 1)
     v.wait_ge(S.ldw1, 16)
     v.quantize_mx(T.w1q[:, 0:128], T.w1s[:, 0:128], T.w1b[:, 0:512]).then_inc(S.qw1a, 1)
     v.quantize_mx(T.w1q[:, 128:256], T.w1s[:, 128:256], T.w1b[:, 512:1024]).then_inc(S.qw1b, 1)
-    v.wait_ge(S.z0, 1)
-    v.tensor_scalar(T.hb[:, 0:4 * NC:4], T.ps[:, 0:NC], 0.0, CF, AluOpType.max, AluOpType.mult).then_inc(S.av, 1)
-    v.tensor_scalar(T.hb[:, 1:4 * NC:4], T.ps[:, 0:NC], -CF, 0.0, AluOpType.mult, AluOpType.max).then_inc(S.av, 1)
-    v.wait_ge(S.av, 2)
-    v.wait_ge(S.as_, 2)
-    v.quantize_mx(T.hq[:, blk(rank)], T.hs[:, blk(rank)], T.hb[:]).then_inc(S.hdone, 1)
+    v.quantize_mx(T.xq[:, HC:NC], T.xs[:, HC:NC], T.xb[:, 4 * HC:4 * NC]).then_inc(S.qx1, 1)
+    for h in (0, 1):
+        c0, c1 = 4 * HC * h, 4 * HC * (h + 1)
+        z0 = T.ps[:, 512 * (2 * h):512 * (2 * h) + HC]
+        v.wait_ge(S["z0%d" % h], 1)
+        v.tensor_scalar(T.hb[:, c0 + 0:c1:4], z0, 0.0, CF, AluOpType.max, AluOpType.mult).then_inc(S["av%d" % h], 1)
+        v.tensor_scalar(T.hb[:, c0 + 1:c1:4], z0, -CF, 0.0, AluOpType.mult, AluOpType.max).then_inc(S["av%d" % h], 1)
+        v.wait_ge(S["av%d" % h], 2)
+        v.wait_ge(S["as%d" % h], 2)
+        w0 = NC * rank + HC * h
+        v.quantize_mx(T.hq[:, w0:w0 + HC], T.hs[:, w0:w0 + HC], T.hb[:, c0:c1]).then_inc(S["h%d" % h], 1)
     v.wait_ge(S.ldw2, 16)
     v.quantize_mx(T.w2q[:], T.w2s[:], T.w2b[:]).then_inc(S.qw2, 1)
 
-    sc.wait_ge(S.z1, 1)
-    sc.activation(T.hb[:, 2:4 * NC:4], T.ps[:, 512:512 + NC], ActivationFunctionType.Relu, scale=CF).then_inc(S.as_, 1)
-    sc.activation(T.hb[:, 3:4 * NC:4], T.ps[:, 512:512 + NC], ActivationFunctionType.Relu, scale=-CF).then_inc(S.as_, 1)
+    for h in (0, 1):
+        c0, c1 = 4 * HC * h, 4 * HC * (h + 1)
+        z1 = T.ps[:, 512 * (2 * h + 1):512 * (2 * h + 1) + HC]
+        sc.wait_ge(S["z1%d" % h], 1)
+        sc.activation(T.hb[:, c0 + 2:c1:4], z1, Relu, scale=CF).then_inc(S["as%d" % h], 1)
+        sc.activation(T.hb[:, c0 + 3:c1:4], z1, Relu, scale=-CF).then_inc(S["as%d" % h], 1)
 
-    te.wait_ge(S.qx, 1)
+    te.wait_ge(S.qx0, 1)
     te.wait_ge(S.qw1a, 1)
-    te.matmul_mx(T.ps[:, 0:NC], T.w1q[:, 0:128], T.w1s[:, 0:128], T.xq[:], T.xs[:], True, True).then_inc(S.z0, 1)
+    te.matmul_mx(T.ps[:, 0:HC], T.w1q[:, 0:128], T.w1s[:, 0:128], T.xq[:, 0:HC], T.xs[:, 0:HC], True, True).then_inc(S.z00, 1)
     te.wait_ge(S.qw1b, 1)
-    te.matmul_mx(T.ps[:, 512:512 + NC], T.w1q[:, 128:256], T.w1s[:, 128:256], T.xq[:], T.xs[:], True, True).then_inc(S.z1, 1)
-    te.wait_ge(S.hdone, 1)
+    te.matmul_mx(T.ps[:, 512:512 + HC], T.w1q[:, 128:256], T.w1s[:, 128:256], T.xq[:, 0:HC], T.xs[:, 0:HC], True, True).then_inc(S.z10, 1)
+    te.wait_ge(S.qx1, 1)
+    te.matmul_mx(T.ps[:, 1024:1024 + HC], T.w1q[:, 0:128], T.w1s[:, 0:128], T.xq[:, HC:NC], T.xs[:, HC:NC], True, True).then_inc(S.z01, 1)
+    te.matmul_mx(T.ps[:, 1536:1536 + HC], T.w1q[:, 128:256], T.w1s[:, 128:256], T.xq[:, HC:NC], T.xs[:, HC:NC], True, True).then_inc(S.z11, 1)
+    te.wait_ge(S.h0, 1)
+    te.wait_ge(S.h1, 1)
     te.wait_ge(S.qw2, 1)
-    seq = order[core]
     bank = {}
     for i, j in enumerate(seq):
-        bank[j] = 512 * ((2 + i) % 8)
+        bank[j] = 512 * ((4 + i) % 8)
         if j != rank:
-            te.wait_ge(S["p%d" % j], got[j])
-            te.wait_ge(S["c%d" % j], got[j])
+            te.wait_ge(S["p%d" % j], got["p", j])
+            te.wait_ge(S["c%d" % j], got["c", j])
         te.matmul_mx(T.ps[:, bank[j]:bank[j] + NC], T.w2q[:], T.w2s[:], T.hq[:, blk(j)], T.hs[:, blk(j)],
                      True, True).then_inc(S["m%d" % j], 1)
 
@@ -129,7 +192,7 @@ def rank_program(g, core, T, topo):
             v.tensor_copy(T.yb[:, blk(j)], T.ps[:, bank[j]:bank[j] + NC]).then_inc(S["e%d" % j], 1)
         else:
             sc.wait_ge(S["m%d" % j], 1)
-            sc.activation(T.yb[:, blk(j)], T.ps[:, bank[j]:bank[j] + NC], ActivationFunctionType.Copy).then_inc(S["e%d" % j], 1)
+            sc.activation(T.yb[:, blk(j)], T.ps[:, bank[j]:bank[j] + NC], Copy).then_inc(S["e%d" % j], 1)
 
     nst = 0
     for i in range(0, N, 2):
@@ -146,17 +209,3 @@ def rank_program(g, core, T, topo):
                 sy.dma_start(T.y[:, blk(j)], T.yb[:, blk(j)]).then_inc(S.st, 16)
                 nst += 1
     sy.wait_ge(S.st, 16 * nst)
-
-    g.wait_ge(S.hdone, 1)
-    total = 0
-    for j, dst in sends[core]:
-        m = _mask(topo, cores, core, dst)
-        rid, pid, _se = topo.addr(dst)
-        if j != rank:
-            g.wait_ge(S["p%d" % j], got[j])
-        g.remote_dma(T.hs[:, blk(j)], T.hs[:, blk(j)], S["p%d" % j], S.sent, pid, rid, m)
-        if j != rank:
-            g.wait_ge(S["c%d" % j], got[j])
-        g.remote_dma(T.hq[:, blk(j)].bitcast(dt.uint8), T.hq[:, blk(j)].bitcast(dt.uint8), S["c%d" % j], S.sent, pid, rid, m)
-        total += 2 * _bits(m)
-    g.wait_ge(S.sent, total)

@@ -23,7 +23,7 @@ SCRATCH = {
     "yb": ("sbuf", [128, N * NC], "float32"),
     "ps": ("psum", [128, 512 * 8], "float32"),
 }
-SEMAPHORES = (["ldx", "ldw1", "ldw2", "qx0", "qx1", "qw1a", "qw1b", "qw2", "z00", "z10", "z01", "z11",
+SEMAPHORES = (["ldx", "ldx1", "ldw1", "ldw2", "qx0", "qx1", "qw1a", "qw1b", "qw2", "z00", "z10", "z01", "z11",
                "av0", "av1", "as0", "as1", "h0", "h1", "sent", "st"]
               + ["c%d" % j for j in range(N)] + ["p%d" % j for j in range(N)]
               + ["m%d" % j for j in range(N)] + ["e%d" % j for j in range(N)])
@@ -56,8 +56,8 @@ def _plan(T, topo):
     ops = {c: [] for c in cores}
     order = {c: [] for c in cores}
 
-    def both(lst, j, src, dst, split=False):
-        m = _masks(topo, cores, src, dst)[0]
+    def both(lst, j, src, dst, split=False, wide=False):
+        m = _masks(topo, cores, src, dst)[1 if wide else 0]
         if split:
             lst.append(("p", j, 0, HC, dst, m))
             lst.append(("p", j, HC, NC, dst, m))
@@ -87,8 +87,11 @@ def _plan(T, topo):
                 src = mem[(k - d) % K]
                 j = T.rank_of(src[s])
                 if d not in DIRECT:
-                    both(ops[c], j, c, other)
-                order[c] += [j, T.rank_of(src[1 - s])]
+                    both(ops[c], j, c, other, wide=(d >= 2))
+                order[c].append(j)
+                if d >= 2:
+                    order[c].append(T.rank_of(mem[(k - d + 1) % K][1 - s]))
+            order[c].append(T.rank_of(mem[(k - K + 1) % K][1 - s]))
     return ops, order
 
 
@@ -136,8 +139,9 @@ def _compute(g, rank, T, seq, got):
     v, sc, te, sy = g.vector, g.scalar, g.tensor, g.sync
     Relu, Copy = ActivationFunctionType.Relu, ActivationFunctionType.Copy
 
-    sy.dma_start(T.xb[:], T.x[:]).then_inc(S.ldx, 16)
+    sy.dma_start(T.xb[:, 0:4 * HC], T.x[:, 0:4 * HC]).then_inc(S.ldx, 16)
     sc.dma_start(T.w1b[:], T.w1[:]).then_inc(S.ldw1, 16)
+    sy.dma_start(T.xb[:, 4 * HC:4 * NC], T.x[:, 4 * HC:4 * NC]).then_inc(S.ldx1, 16)
     sy.dma_start(T.w2b[:], T.w2[:]).then_inc(S.ldw2, 16)
 
     v.wait_ge(S.ldx, 16)
@@ -145,13 +149,15 @@ def _compute(g, rank, T, seq, got):
     v.wait_ge(S.ldw1, 16)
     v.quantize_mx(T.w1q[:, 0:128], T.w1s[:, 0:128], T.w1b[:, 0:512]).then_inc(S.qw1a, 1)
     v.quantize_mx(T.w1q[:, 128:256], T.w1s[:, 128:256], T.w1b[:, 512:1024]).then_inc(S.qw1b, 1)
-    v.quantize_mx(T.xq[:, HC:NC], T.xs[:, HC:NC], T.xb[:, 4 * HC:4 * NC]).then_inc(S.qx1, 1)
     for h in (0, 1):
         c0, c1 = 4 * HC * h, 4 * HC * (h + 1)
         z0 = T.ps[:, 512 * (2 * h):512 * (2 * h) + HC]
         v.wait_ge(S["z0%d" % h], 1)
         v.tensor_scalar(T.hb[:, c0 + 0:c1:4], z0, 0.0, CF, AluOpType.max, AluOpType.mult).then_inc(S["av%d" % h], 1)
         v.tensor_scalar(T.hb[:, c0 + 1:c1:4], z0, -CF, 0.0, AluOpType.mult, AluOpType.max).then_inc(S["av%d" % h], 1)
+        if h == 0:
+            v.wait_ge(S.ldx1, 16)
+            v.quantize_mx(T.xq[:, HC:NC], T.xs[:, HC:NC], T.xb[:, 4 * HC:4 * NC]).then_inc(S.qx1, 1)
         v.wait_ge(S["av%d" % h], 2)
         v.wait_ge(S["as%d" % h], 2)
         w0 = NC * rank + HC * h
@@ -195,17 +201,18 @@ def _compute(g, rank, T, seq, got):
             sc.activation(T.yb[:, blk(j)], T.ps[:, bank[j]:bank[j] + NC], Copy).then_inc(S["e%d" % j], 1)
 
     nst = 0
-    for i in range(0, N, 2):
-        a, b = seq[i], seq[i + 1]
-        lo = min(a, b)
-        if i + 2 < N and abs(a - b) == 1:
-            sy.wait_ge(S["e%d" % a], 1)
-            sy.wait_ge(S["e%d" % b], 1)
+    early = seq[0:3] + [seq[4]]
+    held = []
+    for j in seq:
+        sy.wait_ge(S["e%d" % j], 1)
+        if j in early:
+            pal = [q for q in held if abs(q - j) == 1 and min(q, j) % 2 == 0]
+            if not pal:
+                held.append(j)
+                continue
+            lo = min(j, pal[0])
             sy.dma_start(T.y[:, NC * lo:NC * lo + 2 * NC], T.yb[:, NC * lo:NC * lo + 2 * NC]).then_inc(S.st, 16)
-            nst += 1
         else:
-            for j in (a, b):
-                sy.wait_ge(S["e%d" % j], 1)
-                sy.dma_start(T.y[:, blk(j)], T.yb[:, blk(j)]).then_inc(S.st, 16)
-                nst += 1
+            sy.dma_start(T.y[:, blk(j)], T.yb[:, blk(j)]).then_inc(S.st, 16)
+        nst += 1
     sy.wait_ge(S.st, 16 * nst)

from concourse.mybir import dt, AluOpType, ActivationFunctionType

N = 8
NC = 256
HC = NC // 2
CF = 0.031
DIRECT = ()
HELP = (3,)

SCRATCH = {
    "xb": ("sbuf", [128, 4 * NC], "bfloat16"),
    "w1b": ("sbuf", [128, 1024], "bfloat16"),
    "w2b": ("sbuf", [128, 512], "bfloat16"),
    "xq": ("sbuf", [128, NC], "float8_e4m3fn_x4"),
    "xs": ("sbuf", [128, NC], "uint8"),
    "w1q": ("sbuf", [128, 256], "float8_e4m3fn_x4"),
    "w1s": ("sbuf", [128, 256], "uint8"),
    "w2q": ("sbuf", [128, 128], "float8_e4m3fn_x4"),
    "w2s": ("sbuf", [128, 128], "uint8"),
    "hb": ("sbuf", [128, 4 * NC], "bfloat16"),
    "hq": ("sbuf", [128, N * NC], "float8_e4m3fn_x4"),
    "hs": ("sbuf", [128, N * NC], "uint8"),
    "yb": ("sbuf", [128, N * NC], "float32"),
    "ps": ("psum", [128, 512 * 8], "float32"),
}
SEMAPHORES = (["ldx", "ldx1", "ldw1", "ldw2", "qx0", "qx1", "qw1a", "qw1b", "qw2", "z00", "z10", "z01", "z11",
               "av0", "av1", "as0", "as1", "h0", "h1", "sent", "st"]
              + ["c%d" % j for j in range(N)] + ["p%d" % j for j in range(N)]
              + ["m%d" % j for j in range(N)] + ["e%d" % j for j in range(N)])


def _bits(m):
    return bin(m).count("1")


def _masks(topo, cores, src, dst):
    full = topo.mask(src, dst)
    if topo.chip(src) != topo.chip(dst):
        return full, full
    far = 0
    for c in cores:
        if topo.chip(c) != topo.chip(src):
            far |= topo.mask(src, c)
    rest = full & ~far
    return (rest if _bits(rest) in (1, 2, 4, 8, 16) else full), full


def _plan(T, topo):
    cores = list(T.cores)
    chips = []
    for c in cores:
        if topo.chip(c) not in chips:
            chips.append(topo.chip(c))
    mem = [[c for c in cores if topo.chip(c) == ch] for ch in chips]
    K = len(chips)
    ops = {c: [] for c in cores}
    order = {c: [] for c in cores}

    def both(lst, j, src, dst, split=False, wide=False):
        m = _masks(topo, cores, src, dst)[1 if wide else 0]
        if split:
            lst.append(("p", j, 0, HC, dst, m))
            lst.append(("p", j, HC, NC, dst, m))
        else:
            lst.append(("p", j, 0, NC, dst, m))
        lst.append(("c", j, 0, NC, dst, m))

    for k in range(K):
        for s, c in enumerate(mem[k]):
            other = mem[k][1 - s]
            me = T.rank_of(c)
            hc = None
            if HELP:
                cand = [q for q in range(128) if topo.chip(q) == chips[k] and q not in cores and topo.die(q) != topo.die(c)
                        and all(topo.may_write(q, t) for t in cores)]
                hc = cand[s]
                both(ops[c], me, c, hc, True)
                ops[hc] = []
            for d in range(1, K):
                who = hc if d in HELP else c
                both(ops[who], me, who, mem[(k + d) % K][s])
                if d in DIRECT:
                    both(ops[who], me, who, mem[(k + d) % K][1 - s])
            both(ops[c], me, c, other)
            order[c] += [me, T.rank_of(other)]
            for d in range(1, K):
                src = mem[(k - d) % K]
                j = T.rank_of(src[s])
                if d not in DIRECT:
                    both(ops[c], j, c, other, wide=(d >= 2))
                order[c].append(j)
                if d >= 2:
                    order[c].append(T.rank_of(mem[(k - d + 1) % K][1 - s]))
            order[c].append(T.rank_of(mem[(k - K + 1) % K][1 - s]))
    return ops, order


def rank_program(g, core, T, topo):
    rank = T.rank_of(core)
    S = T.sem
    ops, order = _plan(T, topo)
    if core not in ops:
        return
    got = {}
    for c in ops:
        for kind, j, a, b, dst, m in ops[c]:
            if dst == core:
                got[kind, j] = got.get((kind, j), 0) + _bits(m)
    if rank is not None:
        _compute(g, rank, T, order[core], got)

    total = 0
    seen = set()
    for kind, j, a, b, dst, m in ops[core]:
        if j == rank:
            need = [("h0", 1)] if b <= HC else [("h0", 1), ("h1", 1)]
        else:
            need = [("%s%d" % (kind, j), got[kind, j])]
        for name, val in need:
            if name not in seen:
                g.wait_ge(S[name], val)
                seen.add(name)
        rid, pid, _se = topo.addr(dst)
        cols = slice(NC * j + a, NC * j + b)
        if kind == "p":
            g.remote_dma(T.hs[:, cols], T.hs[:, cols], S["p%d" % j], S.sent, pid, rid, m)
        else:
            g.remote_dma(T.hq[:, cols].bitcast(dt.uint8), T.hq[:, cols].bitcast(dt.uint8), S["c%d" % j], S.sent, pid, rid, m)
        total += _bits(m)
    g.wait_ge(S.sent, total)


def _compute(g, rank, T, seq, got):
    S = T.sem

    def blk(j):
        return slice(NC * j, NC * j + NC)

    v, sc, te, sy = g.vector, g.scalar, g.tensor, g.sync
    Relu, Copy = ActivationFunctionType.Relu, ActivationFunctionType.Copy

    sy.dma_start(T.xb[:, 0:4 * HC], T.x[:, 0:4 * HC]).then_inc(S.ldx, 16)
    sc.dma_start(T.w1b[:], T.w1[:]).then_inc(S.ldw1, 16)
    sy.dma_start(T.xb[:, 4 * HC:4 * NC], T.x[:, 4 * HC:4 * NC]).then_inc(S.ldx1, 16)
    sy.dma_start(T.w2b[:], T.w2[:]).then_inc(S.ldw2, 16)

    v.wait_ge(S.ldx, 16)
    v.quantize_mx(T.xq[:, 0:HC], T.xs[:, 0:HC], T.xb[:, 0:4 * HC]).then_inc(S.qx0, 1)
    v.wait_ge(S.ldw1, 16)
    v.quantize_mx(T.w1q[:, 0:128], T.w1s[:, 0:128], T.w1b[:, 0:512]).then_inc(S.qw1a, 1)
    v.quantize_mx(T.w1q[:, 128:256], T.w1s[:, 128:256], T.w1b[:, 512:1024]).then_inc(S.qw1b, 1)
    for h in (0, 1):
        c0, c1 = 4 * HC * h, 4 * HC * (h + 1)
        z0 = T.ps[:, 512 * (2 * h):512 * (2 * h) + HC]
        v.wait_ge(S["z0%d" % h], 1)
        v.tensor_scalar(T.hb[:, c0 + 0:c1:4], z0, 0.0, CF, AluOpType.max, AluOpType.mult).then_inc(S["av%d" % h], 1)
        v.tensor_scalar(T.hb[:, c0 + 1:c1:4], z0, -CF, 0.0, AluOpType.mult, AluOpType.max).then_inc(S["av%d" % h], 1)
        if h == 0:
            v.wait_ge(S.ldx1, 16)
            v.quantize_mx(T.xq[:, HC:NC], T.xs[:, HC:NC], T.xb[:, 4 * HC:4 * NC]).then_inc(S.qx1, 1)
        v.wait_ge(S["av%d" % h], 2)
        v.wait_ge(S["as%d" % h], 2)
        w0 = NC * rank + HC * h
        v.quantize_mx(T.hq[:, w0:w0 + HC], T.hs[:, w0:w0 + HC], T.hb[:, c0:c1]).then_inc(S["h%d" % h], 1)
    v.wait_ge(S.ldw2, 16)
    v.quantize_mx(T.w2q[:], T.w2s[:], T.w2b[:]).then_inc(S.qw2, 1)

    for h in (0, 1):
        c0, c1 = 4 * HC * h, 4 * HC * (h + 1)
        z1 = T.ps[:, 512 * (2 * h + 1):512 * (2 * h + 1) + HC]
        sc.wait_ge(S["z1%d" % h], 1)
        sc.activation(T.hb[:, c0 + 2:c1:4], z1, Relu, scale=CF).then_inc(S["as%d" % h], 1)
        sc.activation(T.hb[:, c0 + 3:c1:4], z1, Relu, scale=-CF).then_inc(S["as%d" % h], 1)

    te.wait_ge(S.qx0, 1)
    te.wait_ge(S.qw1a, 1)
    te.matmul_mx(T.ps[:, 0:HC], T.w1q[:, 0:128], T.w1s[:, 0:128], T.xq[:, 0:HC], T.xs[:, 0:HC], True, True).then_inc(S.z00, 1)
    te.wait_ge(S.qw1b, 1)
    te.matmul_mx(T.ps[:, 512:512 + HC], T.w1q[:, 128:256], T.w1s[:, 128:256], T.xq[:, 0:HC], T.xs[:, 0:HC], True, True).then_inc(S.z10, 1)
    te.wait_ge(S.qx1, 1)
    te.matmul_mx(T.ps[:, 1024:1024 + HC], T.w1q[:, 0:128], T.w1s[:, 0:128], T.xq[:, HC:NC], T.xs[:, HC:NC], True, True).then_inc(S.z01, 1)
    te.matmul_mx(T.ps[:, 1536:1536 + HC], T.w1q[:, 128:256], T.w1s[:, 128:256], T.xq[:, HC:NC], T.xs[:, HC:NC], True, True).then_inc(S.z11, 1)
    te.wait_ge(S.h0, 1)
    te.wait_ge(S.h1, 1)
    te.wait_ge(S.qw2, 1)
    bank = {}
    for i, j in enumerate(seq):
        bank[j] = 512 * ((4 + i) % 8)
        if j != rank:
            te.wait_ge(S["p%d" % j], got["p", j])
            te.wait_ge(S["c%d" % j], got["c", j])
        te.matmul_mx(T.ps[:, bank[j]:bank[j] + NC], T.w2q[:], T.w2s[:], T.hq[:, blk(j)], T.hs[:, blk(j)],
                     True, True).then_inc(S["m%d" % j], 1)

    for i, j in enumerate(seq):
        if i % 2 == 0:
            v.wait_ge(S["m%d" % j], 1)
            v.tensor_copy(T.yb[:, blk(j)], T.ps[:, bank[j]:bank[j] + NC]).then_inc(S["e%d" % j], 1)
        else:
            sc.wait_ge(S["m%d" % j], 1)
            sc.activation(T.yb[:, blk(j)], T.ps[:, bank[j]:bank[j] + NC], Copy).then_inc(S["e%d" % j], 1)

    nst = 0
    early = seq[0:3] + [seq[4]]
    held = []
    for j in seq:
        sy.wait_ge(S["e%d" % j], 1)
        if j in early:
            pal = [q for q in held if abs(q - j) == 1 and min(q, j) % 2 == 0]
            if not pal:
                held.append(j)
                continue
            lo = min(j, pal[0])
            sy.dma_start(T.y[:, NC * lo:NC * lo + 2 * NC], T.yb[:, NC * lo:NC * lo + 2 * NC]).then_inc(S.st, 16)
        else:
            sy.dma_start(T.y[:, blk(j)], T.yb[:, blk(j)]).then_inc(S.st, 16)
        nst += 1
    sy.wait_ge(S.st, 16 * nst)
